import numpy as np
import ml_dtypes


def mxq(x, axis, fmt="e4m3"):
    dtype, down = {"e4m3": (ml_dtypes.float8_e4m3fn, 7), "e5m2": (ml_dtypes.float8_e5m2, 14)}[fmt]
    v = np.moveaxis(np.asarray(x, np.float32).astype(ml_dtypes.bfloat16).astype(np.float64), axis, -1)
    blocks = v.reshape(v.shape[:-1] + (-1, 32))
    amax = np.abs(blocks).max(-1, keepdims=True)
    byte = np.maximum(np.where(amax > 0, np.frexp(amax)[1] - 1 + 127, 0) - down, 1)
    scale = np.exp2(byte - 127.0)
    codes = (blocks / scale).astype(np.float32).astype(dtype).astype(np.float64)
    return np.moveaxis((codes * scale).reshape(v.shape), -1, axis)


WIDE = False


def mx_kscale(k):
    if not WIDE:
        return np.ones(k)
    levels = np.array([10, -10, 5, -5, 0])
    if k % 512:
        return np.exp2(np.random.permutation(np.resize(levels, k // 32))).repeat(32)
    a = np.empty((k // 512, 16))
    for p in range(k // 512):
        a[p, :8] = np.random.permutation(np.resize(levels, 8))
        for g in range(8):
            far = levels[np.abs(levels - a[p, g]) >= 10]
            a[p, g + 8] = far[np.random.randint(len(far))]
    return np.exp2(a.ravel()).repeat(32)


def f64(x):
    return np.asarray(x).astype(np.float64)


def striped(idx):
    return np.tile(idx.reshape(-1, 16).T, (8, 1)).astype(np.uint16)


def unstriped(offs):
    return offs[:16].T.reshape(-1).astype(np.int64)


E2M1 = np.array([0.0, 0.5, 1.0, 1.5, 2.0, 3.0, 4.0, 6.0, -0.0, -0.5, -1.0, -1.5, -2.0, -3.0, -4.0, -6.0])


def pack_weight(w, fmt):
    k, n = w.shape
    w = f64(np.asarray(w, np.float32).astype(ml_dtypes.bfloat16)).reshape(k // 32, 32, n)
    amax = np.abs(w).max(1)
    if fmt == "e4m3":
        byte = np.frexp(amax)[1] - 1 + 127 - 7
    else:
        mant, ex = np.frexp(amax / 6.0)
        byte = np.where(mant > 0.5, ex, ex - 1) + 127
    byte = np.clip(np.where(amax > 0, byte, 1), 1, 254)
    scaled = (w * np.exp2(127.0 - byte)[:, None, :]).reshape(k, n).astype(np.float32)
    by_word = np.ascontiguousarray(scaled.reshape(k // 512, 128, 4, n).transpose(0, 1, 3, 2))
    if fmt == "e4m3":
        words = by_word.astype(ml_dtypes.float8_e4m3fn).view(np.uint8)
    else:
        c = by_word.astype(ml_dtypes.float4_e2m1fn).view(np.uint8) & 0xF
        words = (c[..., 0::2] | (c[..., 1::2] << 4)).reshape(k // 512, 128, 2 * n)
    return np.ascontiguousarray(words), np.ascontiguousarray(byte.astype(np.uint8).reshape(k // 512, 16, n))


def unpack_weight(words, scales, fmt):
    g, _, n = scales.shape
    words = np.ascontiguousarray(words).reshape(g, 128, n, -1)
    if fmt == "e4m3":
        vals = words.view(ml_dtypes.float8_e4m3fn).astype(np.float64)
    else:
        nib = np.empty((g, 128, n, 4), np.uint8)
        nib[..., 0::2] = words & 0xF
        nib[..., 1::2] = words >> 4
        vals = E2M1[nib]
    vals = vals * np.repeat(np.exp2(scales.astype(np.float64) - 127.0), 8, axis=1)[..., None]
    return vals.transpose(0, 1, 3, 2).reshape(g * 512, n)


def gelu(v):
    return 0.5 * v * (1.0 + np.tanh(np.sqrt(2.0 / np.pi) * (v + 0.044715 * v**3)))


K, T, S, H, T2, P, N = 512, 4096, 1024, 1536, 2048, 1024, 384


def setup_inputs():
    n = np.random.standard_normal
    s = mx_kscale(K)[:, None]
    u = mx_kscale(H)[:, None]
    d = {}
    d["tab_words"], d["tab_scales"] = pack_weight(n((K, T)) * s, "e4m3")
    d["offs"] = striped(np.random.permutation(T)[:S])
    d["offs2"] = striped(np.random.permutation(T2)[:S])
    d["offs3"] = striped(np.random.permutation(T2)[:P])
    d["offs4"] = striped(np.random.permutation(T2)[:P])
    d["w1"] = (3.0 * n((K, H)) / K**0.5 / s).astype(np.float32)
    d["w2_words"], d["w2_scales"] = pack_weight(n((K, H)) / K**0.5 / s, "e2m1")
    d["lift"] = np.random.uniform(1.8, 3.2, H).astype(np.float32)
    d["gain"] = (0.42 * np.exp(0.3 * n(H)) * u[:, 0]).astype(np.float32)
    d["wgs"] = np.exp(0.3 * n((128, S))).astype(np.float32)
    d["page0"] = (0.9 * n((H, T2)) * u).astype(np.float32)
    d["tune"] = np.exp(0.3 * n(H)).astype(np.float32)
    d["w3"] = (0.4 * n((H, N)) / H**0.5 / u).astype(np.float32)
    d["wgo"] = np.exp(0.3 * n((128, P))).astype(np.float32)
    d["page1"] = (0.4 * n((N, T2))).astype(np.float32)
    return d


def reference(tab_words, tab_scales, offs, offs2, offs3, offs4, w1, w2_words, w2_scales,
              lift, gain, wgs, page0, tune, w3, wgo, page1):
    v = unpack_weight(tab_words, tab_scales, "e4m3")[:, unstriped(offs)]
    pitch = mxq(f64(w1), 0, "e4m3").T @ v
    beat = unpack_weight(w2_words, w2_scales, "e2m1").T @ v
    sig = 1.0 / (1.0 + np.exp(-pitch))
    h = f64(gain)[:, None] * np.maximum(pitch, f64(lift)[:, None] * sig - beat)
    page = f64(page0).copy()
    page[:, unstriped(offs2)] = np.tile(f64(wgs), (H // 128, 1)) * h
    x = f64(tune)[:, None] * page[:, unstriped(offs3)]
    y = np.sin(mxq(f64(w3), 0, "e4m3").T @ mxq(x, 0, "e4m3"))
    out = f64(page1).copy()
    out[:, unstriped(offs4)] = np.tile(f64(wgo), (N // 128, 1)) * y
    return out

@@ -1,0 +1,337 @@
+import math
+from contextlib import ExitStack
+
+import concourse.mybir as mybir
+
+K, T, S, H, T2, RECALL, N = 512, 4096, 1024, 1536, 2048, 1024, 384
+FLOPS = 2 * (2 * K * H * S) + 2 * H * N * RECALL
+
+F32 = mybir.dt.float32
+BF16 = mybir.dt.bfloat16
+I32 = mybir.dt.int32
+U32 = mybir.dt.uint32
+U16 = mybir.dt.uint16
+U8 = mybir.dt.uint8
+FP8X4 = mybir.dt.float8_e4m3fn_x4
+FP4X4 = mybir.dt.float4_e2m1fn_x4
+ALU = mybir.AluOpType
+ACT = mybir.ActivationFunctionType
+
+P = 128
+PACK = 4
+PASS = P * PACK
+BANK = 512
+HALVES = S // BANK
+GROUPS = H // PASS
+SLICES = GROUPS * PACK
+LIST_COLS = BANK // 16
+CHUNKS = ((0, 256), (256, 512), (512, 1024))
+W3_STEPS = [5, 6, 9]
+ROUNDER = 1.5 * 2.0**23
+
+
+def tile_list_reed_block_filing_kernel(
+    tc, tab_words, tab_scales, offs, offs2, offs3, offs4, w1, w2_words, w2_scales,
+    lift, gain, wgs, page0, tune, w3, wgo, page1, out,
+):
+    nc = tc.nc
+    with ExitStack() as ctx:
+        lists = ctx.enter_context(tc.tile_pool(name="lists", bufs=1))
+        keep = ctx.enter_context(tc.tile_pool(name="keep", bufs=1))
+        work = ctx.enter_context(tc.tile_pool(name="work", bufs=2))
+        psum = ctx.enter_context(tc.psum_pool(name="psum", bufs=4))
+
+        pick = lists.tile([P, S // 16], U16, name="pick")
+        put = lists.tile([P, S // 16], U16, name="put")
+        recall = lists.tile([P, RECALL // 16], U16, name="recall")
+        filed = lists.tile([P, RECALL // 16], U16, name="filed")
+
+        v_words = [keep.tile([P, BANK], U32, name="v_words%d" % h, align_bytes=64) for h in range(HALVES)]
+        v_scales = [keep.tile([P, BANK], U8, name="v_scales%d" % h, align_bytes=64) for h in range(HALVES)]
+        w1_codes = [keep.tile([P, PASS], U32, name="w1_codes%d" % b, align_bytes=64) for b in range(GROUPS)]
+        w1_scales = [keep.tile([P, PASS], U8, name="w1_scales%d" % b, align_bytes=64) for b in range(GROUPS)]
+        w2_codes = keep.tile([P, 2 * H], U8, name="w2_codes", align_bytes=64)
+        w2_plane = keep.tile([P, H], U8, name="w2_plane", align_bytes=64)
+        w3_codes = [keep.tile([P, N], U32, name="w3_codes%d" % b, align_bytes=64) for b in range(GROUPS)]
+        w3_scales = [keep.tile([P, N], U8, name="w3_scales%d" % b, align_bytes=64) for b in range(GROUPS)]
+        x_codes = {}
+        x_scales = {}
+        for b in range(GROUPS):
+            for h in range(HALVES):
+                x_codes[b, h] = keep.tile([P, BANK], U32, name="x_codes%d_%d" % (b, h), align_bytes=64)
+                x_scales[b, h] = keep.tile([P, BANK], U8, name="x_scales%d_%d" % (b, h), align_bytes=64)
+        lift_sb = keep.tile([P, GROUPS, PACK], F32, name="lift_sb")
+        gain_sb = keep.tile([P, GROUPS, PACK], F32, name="gain_sb")
+        tune_sb = keep.tile([P, GROUPS, PACK], F32, name="tune_sb")
+        wgs_first = keep.tile([P, S], F32, name="wgs_first")
+        wgs_rest = keep.tile([P, PACK - 1, S], F32, name="wgs_rest")
+        wgs_rows = wgs.rearrange("(p t) j -> p t j", t=PACK)
+
+        pages = {}
+
+        def load_page(i):
+            b, t = divmod(i, PACK)
+            pages[i] = work.tile([P, T2], F32, name="page", bufs=6)
+            rows = page0[b * PASS : (b + 1) * PASS, :].rearrange("(p t) c -> p t c", t=PACK)
+            nc.sync.dma_start(out=pages[i][:], in_=rows[:, t, :])
+
+        def load_w1(b, pool):
+            raw = pool.tile([P, PACK, PASS], F32, name="w_raw")
+            nc.sync.dma_start(out=raw[:], in_=w1[:, b * PASS : (b + 1) * PASS].rearrange("(p j) c -> p j c", j=PACK))
+            return raw
+
+        def quantise_w1(b, raw):
+            woven = work.tile([P, PACK * PASS], BF16, name="lifted", bufs=2, align_bytes=64)
+            nc.scalar.copy(
+                out=woven[:].rearrange("p (t m j) -> p m t j", t=PACK, j=PACK),
+                in_=raw[:].rearrange("p j (m t) -> p m t j", t=PACK),
+            )
+            nc.vector.quantize_mx(out=w1_codes[b][:].bitcast(FP8X4), scales=w1_scales[b][:], in_=woven[:])
+
+        def quantise_w1_first(raw, pool):
+            woven = pool.tile([P, PACK * PASS], BF16, name="w_woven", align_bytes=64)
+            dst = woven[:].rearrange("p (t m j) -> p m t j", t=PACK, j=PACK)
+            src = raw[:].rearrange("p j (m t) -> p m t j", t=PACK)
+            for t0, t1 in ((0, 1), (1, 2), (2, PACK)):
+                nc.scalar.copy(out=dst[:, :, t0:t1, :], in_=src[:, :, t0:t1, :])
+                nc.vector.quantize_mx(
+                    out=w1_codes[0][:, t0 * P : t1 * P].bitcast(FP8X4), scales=w1_scales[0][:, t0 * P : t1 * P],
+                    in_=woven[:, t0 * PASS : t1 * PASS],
+                )
+
+        def quantise_w3(b):
+            raw = work.tile([P, PACK, N], F32, name="w_raw")
+            nc.sync.dma_start(out=raw[:], in_=w3[b * PASS : (b + 1) * PASS, :].rearrange("(p j) n -> p j n", j=PACK))
+            woven = work.tile([P, PACK * N], BF16, name="lifted", bufs=2, align_bytes=64)
+            nc.scalar.copy(
+                out=woven[:].rearrange("p (c i j) -> p c j i", i=PACK, j=PACK),
+                in_=raw[:].rearrange("p j (c i) -> p c j i", i=PACK),
+            )
+            for c0, c1 in ((0, 2 * P), (2 * P, N)):
+                nc.vector.quantize_mx(
+                    out=w3_codes[b][:, c0:c1].bitcast(FP8X4),
+                    scales=w3_scales[b][:, c0:c1],
+                    in_=woven[:, PACK * c0 : PACK * c1],
+                )
+
+        with tc.tile_pool(name="head", bufs=1, side="right") as head:
+            table = head.tile([P, T], I32, name="table")
+            table_plane = head.tile([P, T], U8, name="table_plane")
+            nc.gpsimd.memset(table_plane[:].bitcast(I32), 0)
+            for q in range(4):
+                nc.gpsimd.dma_start(
+                    out=table_plane[32 * q : 32 * q + 4, :].bitcast(I32),
+                    in_=tab_scales[0, 4 * q : 4 * q + 4, :].bitcast(I32),
+                )
+            w2_raw = head.tile([P, 2 * H], U8, name="w2_raw")
+            w2_rows = head.tile([P, H], U8, name="w2_rows")
+            w2_plane_raw = head.tile([P, H], U8, name="w2_plane_raw")
+            nc.sync.dma_start(pick[:], offs)
+            for q in range(4):
+                nc.sync.dma_start(
+                    out=w2_rows[32 * q : 32 * q + 4, :].bitcast(I32),
+                    in_=w2_scales[0, 4 * q : 4 * q + 4, :].bitcast(I32),
+                )
+            nc.sync.dma_start(out=w2_raw[:].bitcast(I32), in_=w2_words[0].bitcast(I32))
+            nc.sync.dma_start(out=table[:], in_=tab_words[0].rearrange("p t i -> p (t i)").bitcast(I32))
+            w1_first = load_w1(0, head)
+            nc.sync.dma_start(out=gain_sb[:], in_=gain.rearrange("(b p t) -> p b t", p=P, t=PACK))
+            for q in range(4):
+                nc.sync.dma_start(out=wgs_first[32 * q : 32 * q + 32, :], in_=wgs_rows[:, 0, :])
+            load_page(0)
+            nc.sync.dma_start(put[:], offs2)
+            nc.sync.dma_start(out=lift_sb[:], in_=lift.rearrange("(b p t) -> p b t", p=P, t=PACK))
+            nc.sync.dma_start(recall[:], offs3)
+            nc.sync.dma_start(out=tune_sb[:], in_=tune.rearrange("(b p t) -> p b t", p=P, t=PACK))
+            load_page(1)
+            for q in range(4):
+                nc.sync.dma_start(out=wgs_rest[32 * q : 32 * q + 32, :, :], in_=wgs_rows[:, 1:PACK, :])
+            nc.sync.dma_start(filed[:], offs4)
+
+            nc.vector.memset(w2_plane_raw[:].bitcast(I32), 0)
+            for q in range(4):
+                nc.vector.tensor_copy(
+                    out=w2_plane_raw[32 * q : 32 * q + 4, :].bitcast(I32), in_=w2_rows[32 * q : 32 * q + 4, :].bitcast(I32),
+                )
+            for b in range(GROUPS):
+                cols = slice(2 * b * PASS, 2 * (b + 1) * PASS)
+                nc.vector.tensor_copy(
+                    out=w2_codes[:, cols].rearrange("p (t m e) -> p t m e", t=PACK, e=2),
+                    in_=w2_raw[:, cols].rearrange("p (m t e) -> p t m e", t=PACK, e=2),
+                )
+                cols = slice(b * PASS, (b + 1) * PASS)
+                nc.vector.tensor_copy(
+                    out=w2_plane[:, cols].rearrange("p (t m) -> p t m", t=PACK),
+                    in_=w2_plane_raw[:, cols].rearrange("p (m t) -> p t m", t=PACK),
+                )
+
+            for h in range(HALVES):
+                part = pick[:, h * LIST_COLS : (h + 1) * LIST_COLS]
+                nc.vector.tensor_copy(out=v_words[h][:], in_=table[:].bitcast(U32).indirect(part))
+                nc.vector.tensor_copy(out=v_scales[h][:], in_=table_plane[:].indirect(part))
+                if h == 0:
+                    quantise_w1_first(w1_first, head)
+
+        late = ctx.enter_context(tc.tile_pool(name="late", bufs=1, side="right"))
+        filing = [late.tile([P, T2], F32, name="filing%d" % n) for n in range(N // P)]
+        wgo_sb = late.tile([P, RECALL], F32, name="wgo_sb")
+
+        readings = {}
+
+        def read(i):
+            b, t = divmod(i, PACK)
+            for h in range(HALVES):
+                pitch = psum.tile([P, BANK], F32, name="pitch")
+                beat = psum.tile([P, BANK], F32, name="beat")
+                nc.tensor.matmul_mx(
+                    out=pitch[:],
+                    lhsT=w1_codes[b][:, t * P : (t + 1) * P].bitcast(FP8X4),
+                    lhsT_scale=w1_scales[b][:, t * P : (t + 1) * P],
+                    rhs=v_words[h][:].bitcast(FP8X4), rhs_scale=v_scales[h][:],
+                    start=True, stop=True,
+                )
+                nc.tensor.matmul_mx(
+                    out=beat[:],
+                    lhsT=w2_codes[:, 2 * i * P : 2 * (i + 1) * P].bitcast(FP4X4),
+                    lhsT_scale=w2_plane[:, i * P : (i + 1) * P],
+                    rhs=v_words[h][:].bitcast(FP8X4), rhs_scale=v_scales[h][:],
+                    start=True, stop=True,
+                )
+                sig = work.tile([P, BANK], F32, name="sig", bufs=4)
+                nc.scalar.activation(out=sig[:], in_=pitch[:], func=ACT.Sigmoid)
+                readings[i, h] = (pitch, beat, sig)
+            weight = work.tile([P, S], F32, name="weight")
+            dealt = wgs_first[:] if t == 0 else wgs_rest[:, t - 1, :]
+            nc.scalar.activation(out=weight[:], in_=dealt, func=ACT.Copy, scale=gain_sb[:, b, t : t + 1])
+            readings[i] = weight
+
+        def combine(i):
+            b, t = divmod(i, PACK)
+            larger = work.tile([P, S], F32, name="larger", bufs=1)
+            lifted = work.tile([P, S + BANK], F32, name="lifted", bufs=2, align_bytes=64)
+            for h in range(HALVES):
+                pitch, beat, sig = readings[i, h]
+                nc.vector.scalar_tensor_tensor(
+                    out=lifted[:, h * S : h * S + BANK], in0=sig[:], scalar=lift_sb[:, b, t : t + 1], in1=beat[:],
+                    op0=ALU.mult, op1=ALU.subtract,
+                )
+            for h in range(HALVES):
+                nc.vector.tensor_tensor(
+                    out=larger[:, h * BANK : (h + 1) * BANK], in0=readings[i, h][0][:],
+                    in1=lifted[:, h * S : h * S + BANK], op=ALU.max,
+                )
+            return larger, lifted
+
+        def replace(i, larger):
+            nc.vector.tensor_tensor(
+                out=pages[i][:].indirect(put[:]), in0=larger[:], in1=readings[i][:], op=ALU.mult,
+            )
+
+        planes = {}
+
+        def fetch(i, fetched, c0, c1):
+            b, t = divmod(i, PACK)
+            if t == 0 and c0 == 0:
+                planes[b] = work.tile([P, PACK, RECALL], BF16, name="planes")
+            part = recall[:, c0 // 16 : c1 // 16]
+            nc.vector.tensor_copy(out=fetched, in_=pages[i][:].indirect(part))
+            nc.scalar.activation(
+                out=planes[b][:, t, c0:c1], in_=fetched, func=ACT.Copy, scale=tune_sb[:, b, t : t + 1],
+            )
+
+        def fetch_now(i, spent):
+            width = CHUNKS[0][1] if i >= SLICES - PACK else RECALL
+            fetch(i, spent[:, 0:width], 0, width)
+
+        def quantise_x(b, c0, c1, pool, tag):
+            h, lo = divmod(c0, BANK)
+            width = c1 - c0
+            woven = pool.tile([P, PACK * width], BF16, name=tag, align_bytes=64)
+            nc.scalar.copy(
+                out=woven[:].rearrange("p (c i t) -> p c t i", i=PACK, t=PACK),
+                in_=planes[b][:, :, c0:c1].rearrange("p t (c i) -> p c t i", i=PACK),
+            )
+            nc.vector.quantize_mx(
+                out=x_codes[b, h][:, lo : lo + width].bitcast(FP8X4), scales=x_scales[b, h][:, lo : lo + width],
+                in_=woven[:],
+            )
+
+        def reduce_scores(n, c0, c1, bank, tag, bufs):
+            h, lo = divmod(c0, BANK)
+            width = c1 - c0
+            z = psum.tile([P, width], F32, name=bank)
+            for b in range(GROUPS):
+                nc.tensor.matmul_mx(
+                    out=z[:],
+                    lhsT=w3_codes[b][:, n * P : (n + 1) * P].bitcast(FP8X4),
+                    lhsT_scale=w3_scales[b][:, n * P : (n + 1) * P],
+                    rhs=x_codes[b, h][:, lo : lo + width].bitcast(FP8X4), rhs_scale=x_scales[b, h][:, lo : lo + width],
+                    start=(b == 0), stop=(b == GROUPS - 1),
+                )
+            turns_raw = late.tile([P, width], U32, name="turns_raw", bufs=2)
+            nc.scalar.activation(out=turns_raw[:], in_=z[:], func=ACT.Copy, scale=1.0 / (2.0 * math.pi), bias=ROUNDER)
+            turns = late.tile([P, width], F32, name=tag, bufs=bufs)
+            nc.scalar.activation(out=turns[:], in_=turns_raw[:], func=ACT.Copy, bias=-ROUNDER)
+            rest = late.tile([P, width], F32, name="rest", bufs=3)
+            nc.vector.scalar_tensor_tensor(
+                out=rest[:], in0=z[:], scalar=1.0 / (2.0 * math.pi), in1=turns[:], op0=ALU.mult, op1=ALU.subtract,
+            )
+            return rest
+
+        def file_scores(n, c0, c1, rest):
+            y = late.tile([P, c1 - c0], F32, name="y", bufs=3)
+            nc.scalar.activation(out=y[:], in_=rest[:], func=ACT.Sin, scale=2.0 * math.pi)
+            nc.vector.tensor_tensor(
+                out=filing[n][:].indirect(filed[:, c0 // 16 : c1 // 16]),
+                in0=y[:], in1=wgo_sb[:, c0:c1], op=ALU.mult,
+            )
+
+        read(0)
+        for i in range(SLICES):
+            b, t = divmod(i, PACK)
+            if i + 2 < SLICES:
+                load_page(i + 2)
+            if t == PACK - 1 and b + 1 < GROUPS:
+                quantise_w1(b + 1, load_w1(b + 1, work))
+            if i in W3_STEPS:
+                quantise_w3(W3_STEPS.index(i))
+            if i + 1 < SLICES:
+                read(i + 1)
+            larger, lifted = combine(i)
+            if i > 0:
+                fetch_now(i - 1, lifted)
+            replace(i, larger)
+            if t == 0 and b > 0:
+                for h in range(HALVES):
+                    quantise_x(b - 1, h * BANK, (h + 1) * BANK, work, "x_woven")
+            if t == 2:
+                nc.sync.dma_start(out=filing[b][:], in_=page1[b * P : (b + 1) * P, :])
+            if i == PACK - 1:
+                nc.sync.dma_start(out=wgo_sb[:], in_=wgo)
+
+        last = GROUPS - 1
+        fetched = work.tile([P, S + BANK], F32, name="lifted", bufs=2, align_bytes=64)
+        fetch_now(SLICES - 1, fetched)
+        first, second, third = CHUNKS
+        quantise_x(last, *first, late, "first_woven")
+        held = work.tile([P, PACK, second[1] - second[0]], F32, name="larger", bufs=1)
+        for t in range(PACK):
+            fetch(last * PACK + t, held[:, t, :], *second)
+        held = late.tile([P, 2, third[1] - third[0]], F32, name="first_woven", align_bytes=64)
+        for t in range(2):
+            fetch(last * PACK + t, held[:, t, :], *third)
+        scores = [(n, c0, c1) for c0, c1 in CHUNKS for n in range(N // P)]
+        banks = ("pitch", "beat")
+        rest = reduce_scores(*scores[0], banks[0], "first_turns", 1)
+        quantise_x(last, *second, work, "x_woven")
+        held = late.tile([P, 2, third[1] - third[0]], F32, name="first_turns")
+        for t in range(2):
+            fetch(last * PACK + 2 + t, held[:, t, :], *third)
+        for g, (n, c0, c1) in enumerate(scores):
+            if g == N // P - 1:
+                quantise_x(last, *third, work, "x_woven")
+            ahead = reduce_scores(*scores[g + 1], banks[(g + 1) % 2], "turns", 2) if g + 1 < len(scores) else None
+            file_scores(n, c0, c1, rest)
+            if c1 == RECALL:
+                nc.sync.dma_start(out=out[n * P : (n + 1) * P, :], in_=filing[n][:])
+            rest = ahead

@@ -26,7 +26,6 @@ GROUPS = H // PASS
 SLICES = GROUPS * PACK
 LIST_COLS = BANK // 16
 CHUNKS = ((0, 256), (256, 512), (512, 1024))
-W3_STEPS = [5, 6, 9]
 ROUNDER = 1.5 * 2.0**23
 
 
@@ -38,7 +37,6 @@ def tile_list_reed_block_filing_kernel(
     with ExitStack() as ctx:
         lists = ctx.enter_context(tc.tile_pool(name="lists", bufs=1))
         keep = ctx.enter_context(tc.tile_pool(name="keep", bufs=1))
-        work = ctx.enter_context(tc.tile_pool(name="work", bufs=2))
         psum = ctx.enter_context(tc.psum_pool(name="psum", bufs=4))
 
         pick = lists.tile([P, S // 16], U16, name="pick")
@@ -60,11 +58,6 @@ def tile_list_reed_block_filing_kernel(
             for h in range(HALVES):
                 x_codes[b, h] = keep.tile([P, BANK], U32, name="x_codes%d_%d" % (b, h), align_bytes=64)
                 x_scales[b, h] = keep.tile([P, BANK], U8, name="x_scales%d_%d" % (b, h), align_bytes=64)
-        lift_sb = keep.tile([P, GROUPS, PACK], F32, name="lift_sb")
-        gain_sb = keep.tile([P, GROUPS, PACK], F32, name="gain_sb")
-        tune_sb = keep.tile([P, GROUPS, PACK], F32, name="tune_sb")
-        wgs_first = keep.tile([P, S], F32, name="wgs_first")
-        wgs_rest = keep.tile([P, PACK - 1, S], F32, name="wgs_rest")
         wgs_rows = wgs.rearrange("(p t) j -> p t j", t=PACK)
 
         pages = {}
@@ -81,7 +74,7 @@ def tile_list_reed_block_filing_kernel(
             return raw
 
         def quantise_w1(b, raw):
-            woven = work.tile([P, PACK * PASS], BF16, name="lifted", bufs=2, align_bytes=64)
+            woven = work.tile([P, PACK * PASS], BF16, name="x_woven", align_bytes=64)
             nc.scalar.copy(
                 out=woven[:].rearrange("p (t m j) -> p m t j", t=PACK, j=PACK),
                 in_=raw[:].rearrange("p j (m t) -> p m t j", t=PACK),
@@ -99,10 +92,13 @@ def tile_list_reed_block_filing_kernel(
                     in_=woven[:, t0 * PASS : t1 * PASS],
                 )
 
-        def quantise_w3(b):
+        def load_w3(b):
             raw = work.tile([P, PACK, N], F32, name="w_raw")
             nc.sync.dma_start(out=raw[:], in_=w3[b * PASS : (b + 1) * PASS, :].rearrange("(p j) n -> p j n", j=PACK))
-            woven = work.tile([P, PACK * N], BF16, name="lifted", bufs=2, align_bytes=64)
+            return raw
+
+        def quantise_w3(b, raw):
+            woven = work.tile([P, PACK * N], BF16, name="x_woven", align_bytes=64)
             nc.scalar.copy(
                 out=woven[:].rearrange("p (c i j) -> p c j i", i=PACK, j=PACK),
                 in_=raw[:].rearrange("p j (c i) -> p c j i", i=PACK),
@@ -117,42 +113,49 @@ def tile_list_reed_block_filing_kernel(
         with tc.tile_pool(name="head", bufs=1, side="right") as head:
             table = head.tile([P, T], I32, name="table")
             table_plane = head.tile([P, T], U8, name="table_plane")
-            nc.gpsimd.memset(table_plane[:].bitcast(I32), 0)
-            for q in range(4):
-                nc.gpsimd.dma_start(
-                    out=table_plane[32 * q : 32 * q + 4, :].bitcast(I32),
-                    in_=tab_scales[0, 4 * q : 4 * q + 4, :].bitcast(I32),
-                )
             w2_raw = head.tile([P, 2 * H], U8, name="w2_raw")
-            w2_rows = head.tile([P, H], U8, name="w2_rows")
             w2_plane_raw = head.tile([P, H], U8, name="w2_plane_raw")
-            nc.sync.dma_start(pick[:], offs)
-            for q in range(4):
-                nc.sync.dma_start(
-                    out=w2_rows[32 * q : 32 * q + 4, :].bitcast(I32),
-                    in_=w2_scales[0, 4 * q : 4 * q + 4, :].bitcast(I32),
-                )
-            nc.sync.dma_start(out=w2_raw[:].bitcast(I32), in_=w2_words[0].bitcast(I32))
-            nc.sync.dma_start(out=table[:], in_=tab_words[0].rearrange("p t i -> p (t i)").bitcast(I32))
-            w1_first = load_w1(0, head)
+            nc.vector.memset(table_plane[:].bitcast(I32), 0)
+            nc.vector.memset(w2_plane_raw[:].bitcast(I32), 0)
+            with tc.tile_pool(name="staged", bufs=1) as staged:
+                table_rows = staged.tile([P, T // 4], I32, name="table_rows")
+                nc.sync.dma_start(pick[:], offs)
+                for q in range(4):
+                    nc.sync.dma_start(
+                        out=table_rows[32 * q : 32 * q + 4, :], in_=tab_scales[0, 4 * q : 4 * q + 4, :].bitcast(I32),
+                    )
+                nc.sync.dma_start(out=w2_raw[:].bitcast(I32), in_=w2_words[0].bitcast(I32))
+                nc.sync.dma_start(out=table[:], in_=tab_words[0].rearrange("p t i -> p (t i)").bitcast(I32))
+                w1_first = load_w1(0, head)
+                for sb, listed in ((put, offs2), (recall, offs3), (filed, offs4)):
+                    nc.sync.dma_start(sb[:], listed)
+                for q in range(4):
+                    nc.sync.dma_start(
+                        out=w2_plane_raw[32 * q : 32 * q + 4, :].bitcast(I32),
+                        in_=w2_scales[0, 4 * q : 4 * q + 4, :].bitcast(I32),
+                    )
+                for q in range(4):
+                    nc.vector.tensor_copy(
+                        out=table_plane[32 * q : 32 * q + 4, :].bitcast(I32), in_=table_rows[32 * q : 32 * q + 4, :],
+                    )
+
+            work = ctx.enter_context(tc.tile_pool(name="work", bufs=2))
+            lift_sb = work.tile([P, GROUPS, PACK], F32, name="lift_sb", bufs=1)
+            gain_sb = work.tile([P, GROUPS, PACK], F32, name="gain_sb", bufs=1)
+            tune_sb = work.tile([P, GROUPS, PACK], F32, name="tune_sb", bufs=1)
+            wgs_first = work.tile([P, S], F32, name="wgs_first", bufs=1)
+            wgs_rest = work.tile([P, PACK - 1, S], F32, name="wgs_rest", bufs=1)
             nc.sync.dma_start(out=gain_sb[:], in_=gain.rearrange("(b p t) -> p b t", p=P, t=PACK))
             for q in range(4):
                 nc.sync.dma_start(out=wgs_first[32 * q : 32 * q + 32, :], in_=wgs_rows[:, 0, :])
-            load_page(0)
-            nc.sync.dma_start(put[:], offs2)
             nc.sync.dma_start(out=lift_sb[:], in_=lift.rearrange("(b p t) -> p b t", p=P, t=PACK))
-            nc.sync.dma_start(recall[:], offs3)
+            load_page(0)
             nc.sync.dma_start(out=tune_sb[:], in_=tune.rearrange("(b p t) -> p b t", p=P, t=PACK))
             load_page(1)
+            raws = {1: load_w1(1, work)}
             for q in range(4):
                 nc.sync.dma_start(out=wgs_rest[32 * q : 32 * q + 32, :, :], in_=wgs_rows[:, 1:PACK, :])
-            nc.sync.dma_start(filed[:], offs4)
 
-            nc.vector.memset(w2_plane_raw[:].bitcast(I32), 0)
-            for q in range(4):
-                nc.vector.tensor_copy(
-                    out=w2_plane_raw[32 * q : 32 * q + 4, :].bitcast(I32), in_=w2_rows[32 * q : 32 * q + 4, :].bitcast(I32),
-                )
             for b in range(GROUPS):
                 cols = slice(2 * b * PASS, 2 * (b + 1) * PASS)
                 nc.vector.tensor_copy(
@@ -180,6 +183,10 @@ def tile_list_reed_block_filing_kernel(
 
         def read(i):
             b, t = divmod(i, PACK)
+            sig = work.tile([P, S], F32, name="sig", bufs=1)
+            if i > 0:
+                beat_sb = work.tile([P, S], F32, name="beat_sb")
+            lifted = work.tile([P, S + BANK], F32, name="lifted", bufs=3, align_bytes=64)
             for h in range(HALVES):
                 pitch = psum.tile([P, BANK], F32, name="pitch")
                 beat = psum.tile([P, BANK], F32, name="beat")
@@ -197,27 +204,40 @@ def tile_list_reed_block_filing_kernel(
                     rhs=v_words[h][:].bitcast(FP8X4), rhs_scale=v_scales[h][:],
                     start=True, stop=True,
                 )
-                sig = work.tile([P, BANK], F32, name="sig", bufs=4)
-                nc.scalar.activation(out=sig[:], in_=pitch[:], func=ACT.Sigmoid)
-                readings[i, h] = (pitch, beat, sig)
+                nc.scalar.activation(out=sig[:, h * BANK : (h + 1) * BANK], in_=pitch[:], func=ACT.Sigmoid)
+                readings[i, h] = pitch
+                if i == 0:
+                    nc.vector.scalar_tensor_tensor(
+                        out=lifted[:, h * S : h * S + BANK], in0=sig[:, h * BANK : (h + 1) * BANK],
+                        scalar=lift_sb[:, b, t : t + 1], in1=beat[:], op0=ALU.mult, op1=ALU.subtract,
+                    )
+                else:
+                    nc.scalar.copy(out=beat_sb[:, h * BANK : (h + 1) * BANK], in_=beat[:])
+            if i > 0:
+                raised = work.tile([P, S], F32, name="raised")
+                nc.scalar.activation(out=raised[:], in_=sig[:], func=ACT.Copy, scale=lift_sb[:, b, t : t + 1])
+                nc.gpsimd.tensor_tensor(
+                    out=lifted[:].rearrange("p (h c) -> p h c", c=BANK)[:, 0:3:2, :],
+                    in0=raised[:].rearrange("p (h c) -> p h c", c=BANK),
+                    in1=beat_sb[:].rearrange("p (h c) -> p h c", c=BANK), op=ALU.subtract,
+                )
+            readings[i, "lifted"] = lifted
             weight = work.tile([P, S], F32, name="weight")
             dealt = wgs_first[:] if t == 0 else wgs_rest[:, t - 1, :]
-            nc.scalar.activation(out=weight[:], in_=dealt, func=ACT.Copy, scale=gain_sb[:, b, t : t + 1])
+            if i < 2:
+                nc.vector.tensor_scalar(
+                    out=weight[:], in0=dealt, scalar1=gain_sb[:, b, t : t + 1], scalar2=None, op0=ALU.mult,
+                )
+            else:
+                nc.scalar.activation(out=weight[:], in_=dealt, func=ACT.Copy, scale=gain_sb[:, b, t : t + 1])
             readings[i] = weight
 
         def combine(i):
-            b, t = divmod(i, PACK)
             larger = work.tile([P, S], F32, name="larger", bufs=1)
-            lifted = work.tile([P, S + BANK], F32, name="lifted", bufs=2, align_bytes=64)
-            for h in range(HALVES):
-                pitch, beat, sig = readings[i, h]
-                nc.vector.scalar_tensor_tensor(
-                    out=lifted[:, h * S : h * S + BANK], in0=sig[:], scalar=lift_sb[:, b, t : t + 1], in1=beat[:],
-                    op0=ALU.mult, op1=ALU.subtract,
-                )
+            lifted = readings[i, "lifted"]
             for h in range(HALVES):
                 nc.vector.tensor_tensor(
-                    out=larger[:, h * BANK : (h + 1) * BANK], in0=readings[i, h][0][:],
+                    out=larger[:, h * BANK : (h + 1) * BANK], in0=readings[i, h][:],
                     in1=lifted[:, h * S : h * S + BANK], op=ALU.max,
                 )
             return larger, lifted
@@ -256,7 +276,7 @@ def tile_list_reed_block_filing_kernel(
                 in_=woven[:],
             )
 
-        def reduce_scores(n, c0, c1, bank, tag, bufs):
+        def reduce_scores(n, c0, c1, bank, pool, tag):
             h, lo = divmod(c0, BANK)
             width = c1 - c0
             z = psum.tile([P, width], F32, name=bank)
@@ -268,9 +288,9 @@ def tile_list_reed_block_filing_kernel(
                     rhs=x_codes[b, h][:, lo : lo + width].bitcast(FP8X4), rhs_scale=x_scales[b, h][:, lo : lo + width],
                     start=(b == 0), stop=(b == GROUPS - 1),
                 )
-            turns_raw = late.tile([P, width], U32, name="turns_raw", bufs=2)
+            turns_raw = work.tile([P, width], U32, name="raised")
             nc.scalar.activation(out=turns_raw[:], in_=z[:], func=ACT.Copy, scale=1.0 / (2.0 * math.pi), bias=ROUNDER)
-            turns = late.tile([P, width], F32, name=tag, bufs=bufs)
+            turns = pool.tile([P, width], F32, name=tag)
             nc.scalar.activation(out=turns[:], in_=turns_raw[:], func=ACT.Copy, bias=-ROUNDER)
             rest = late.tile([P, width], F32, name="rest", bufs=3)
             nc.vector.scalar_tensor_tensor(
@@ -279,38 +299,52 @@ def tile_list_reed_block_filing_kernel(
             return rest
 
         def file_scores(n, c0, c1, rest):
-            y = late.tile([P, c1 - c0], F32, name="y", bufs=3)
+            y = work.tile([P, c1 - c0], F32, name="weight")
             nc.scalar.activation(out=y[:], in_=rest[:], func=ACT.Sin, scale=2.0 * math.pi)
             nc.vector.tensor_tensor(
                 out=filing[n][:].indirect(filed[:, c0 // 16 : c1 // 16]),
                 in0=y[:], in1=wgo_sb[:, c0:c1], op=ALU.mult,
             )
 
+        loads = {
+            2: lambda: load_w3(0),
+            3: lambda: load_w3(1),
+            4: lambda: load_w1(2, work),
+            7: lambda: load_w3(2),
+        }
+        jobs = {
+            1: lambda: quantise_w1(1, raws[1]),
+            2: lambda: quantise_w3(0, raws[2]),
+            3: lambda: quantise_w3(1, raws[3]),
+            4: lambda: quantise_w1(2, raws[4]),
+            5: lambda: quantise_x(0, 0, BANK, work, "x_woven"),
+            6: lambda: quantise_x(0, BANK, RECALL, work, "x_woven"),
+            7: lambda: quantise_w3(2, raws[7]),
+            9: lambda: quantise_x(1, 0, BANK, work, "x_woven"),
+            10: lambda: quantise_x(1, BANK, RECALL, work, "x_woven"),
+        }
         read(0)
         for i in range(SLICES):
             b, t = divmod(i, PACK)
+            if i + 1 in loads:
+                raws[i + 1] = loads[i + 1]()
             if i + 2 < SLICES:
                 load_page(i + 2)
-            if t == PACK - 1 and b + 1 < GROUPS:
-                quantise_w1(b + 1, load_w1(b + 1, work))
-            if i in W3_STEPS:
-                quantise_w3(W3_STEPS.index(i))
             if i + 1 < SLICES:
                 read(i + 1)
+            if i in jobs:
+                jobs[i]()
             larger, lifted = combine(i)
             if i > 0:
                 fetch_now(i - 1, lifted)
             replace(i, larger)
-            if t == 0 and b > 0:
-                for h in range(HALVES):
-                    quantise_x(b - 1, h * BANK, (h + 1) * BANK, work, "x_woven")
             if t == 2:
                 nc.sync.dma_start(out=filing[b][:], in_=page1[b * P : (b + 1) * P, :])
             if i == PACK - 1:
                 nc.sync.dma_start(out=wgo_sb[:], in_=wgo)
 
         last = GROUPS - 1
-        fetched = work.tile([P, S + BANK], F32, name="lifted", bufs=2, align_bytes=64)
+        fetched = work.tile([P, S + BANK], F32, name="lifted", bufs=3, align_bytes=64)
         fetch_now(SLICES - 1, fetched)
         first, second, third = CHUNKS
         quantise_x(last, *first, late, "first_woven")
@@ -322,7 +356,7 @@ def tile_list_reed_block_filing_kernel(
             fetch(last * PACK + t, held[:, t, :], *third)
         scores = [(n, c0, c1) for c0, c1 in CHUNKS for n in range(N // P)]
         banks = ("pitch", "beat")
-        rest = reduce_scores(*scores[0], banks[0], "first_turns", 1)
+        rest = reduce_scores(*scores[0], banks[0], late, "first_turns")
         quantise_x(last, *second, work, "x_woven")
         held = late.tile([P, 2, third[1] - third[0]], F32, name="first_turns")
         for t in range(2):
@@ -330,7 +364,7 @@ def tile_list_reed_block_filing_kernel(
         for g, (n, c0, c1) in enumerate(scores):
             if g == N // P - 1:
                 quantise_x(last, *third, work, "x_woven")
-            ahead = reduce_scores(*scores[g + 1], banks[(g + 1) % 2], "turns", 2) if g + 1 < len(scores) else None
+            ahead = reduce_scores(*scores[g + 1], banks[(g + 1) % 2], work, "beat_sb") if g + 1 < len(scores) else None
             file_scores(n, c0, c1, rest)
             if c1 == RECALL:
                 nc.sync.dma_start(out=out[n * P : (n + 1) * P, :], in_=filing[n][:])

@@ -26,6 +26,8 @@ GROUPS = H // PASS
 SLICES = GROUPS * PACK
 LIST_COLS = BANK // 16
 CHUNKS = ((0, 256), (256, 512), (512, 1024))
+EARLY = 2
+ROOM = 384
 ROUNDER = 1.5 * 2.0**23
 
 
@@ -37,6 +39,7 @@ def tile_list_reed_block_filing_kernel(
     with ExitStack() as ctx:
         lists = ctx.enter_context(tc.tile_pool(name="lists", bufs=1))
         keep = ctx.enter_context(tc.tile_pool(name="keep", bufs=1))
+        work = ctx.enter_context(tc.tile_pool(name="work", bufs=2))
         psum = ctx.enter_context(tc.psum_pool(name="psum", bufs=4))
 
         pick = lists.tile([P, S // 16], U16, name="pick")
@@ -58,13 +61,19 @@ def tile_list_reed_block_filing_kernel(
             for h in range(HALVES):
                 x_codes[b, h] = keep.tile([P, BANK], U32, name="x_codes%d_%d" % (b, h), align_bytes=64)
                 x_scales[b, h] = keep.tile([P, BANK], U8, name="x_scales%d_%d" % (b, h), align_bytes=64)
+        lift_sb = keep.tile([P, GROUPS, PACK], F32, name="lift_sb")
+        gain_sb = keep.tile([P, GROUPS, PACK], F32, name="gain_sb")
+        tune_sb = keep.tile([P, GROUPS, PACK], F32, name="tune_sb")
+        wgs_first = keep.tile([P, S], F32, name="wgs_first")
+        wgs_rest = keep.tile([P, PACK - 1, S], F32, name="wgs_rest")
+        scratch = [keep.tile([P, 2 * S + BANK], F32, name="scratch%d" % s, align_bytes=64) for s in range(2)]
         wgs_rows = wgs.rearrange("(p t) j -> p t j", t=PACK)
 
         pages = {}
 
         def load_page(i):
             b, t = divmod(i, PACK)
-            pages[i] = work.tile([P, T2], F32, name="page", bufs=6)
+            pages[i] = work.tile([P, T2], F32, name="page", bufs=5)
             rows = page0[b * PASS : (b + 1) * PASS, :].rearrange("(p t) c -> p t c", t=PACK)
             nc.sync.dma_start(out=pages[i][:], in_=rows[:, t, :])
 
@@ -73,8 +82,7 @@ def tile_list_reed_block_filing_kernel(
             nc.sync.dma_start(out=raw[:], in_=w1[:, b * PASS : (b + 1) * PASS].rearrange("(p j) c -> p j c", j=PACK))
             return raw
 
-        def quantise_w1(b, raw):
-            woven = work.tile([P, PACK * PASS], BF16, name="x_woven", align_bytes=64)
+        def quantise_w1(b, raw, woven):
             nc.scalar.copy(
                 out=woven[:].rearrange("p (t m j) -> p m t j", t=PACK, j=PACK),
                 in_=raw[:].rearrange("p j (m t) -> p m t j", t=PACK),
@@ -97,8 +105,8 @@ def tile_list_reed_block_filing_kernel(
             nc.sync.dma_start(out=raw[:], in_=w3[b * PASS : (b + 1) * PASS, :].rearrange("(p j) n -> p j n", j=PACK))
             return raw
 
-        def quantise_w3(b, raw):
-            woven = work.tile([P, PACK * N], BF16, name="x_woven", align_bytes=64)
+        def quantise_w3(b, raw, room):
+            woven = room[:, 0 : PACK * N]
             nc.scalar.copy(
                 out=woven[:].rearrange("p (c i j) -> p c j i", i=PACK, j=PACK),
                 in_=raw[:].rearrange("p j (c i) -> p c j i", i=PACK),
@@ -117,45 +125,38 @@ def tile_list_reed_block_filing_kernel(
             w2_plane_raw = head.tile([P, H], U8, name="w2_plane_raw")
             nc.vector.memset(table_plane[:].bitcast(I32), 0)
             nc.vector.memset(w2_plane_raw[:].bitcast(I32), 0)
-            with tc.tile_pool(name="staged", bufs=1) as staged:
-                table_rows = staged.tile([P, T // 4], I32, name="table_rows")
-                nc.sync.dma_start(pick[:], offs)
-                for q in range(4):
-                    nc.sync.dma_start(
-                        out=table_rows[32 * q : 32 * q + 4, :], in_=tab_scales[0, 4 * q : 4 * q + 4, :].bitcast(I32),
-                    )
-                nc.sync.dma_start(out=w2_raw[:].bitcast(I32), in_=w2_words[0].bitcast(I32))
-                nc.sync.dma_start(out=table[:], in_=tab_words[0].rearrange("p t i -> p (t i)").bitcast(I32))
-                w1_first = load_w1(0, head)
-                for sb, listed in ((put, offs2), (recall, offs3), (filed, offs4)):
-                    nc.sync.dma_start(sb[:], listed)
-                for q in range(4):
-                    nc.sync.dma_start(
-                        out=w2_plane_raw[32 * q : 32 * q + 4, :].bitcast(I32),
-                        in_=w2_scales[0, 4 * q : 4 * q + 4, :].bitcast(I32),
-                    )
-                for q in range(4):
-                    nc.vector.tensor_copy(
-                        out=table_plane[32 * q : 32 * q + 4, :].bitcast(I32), in_=table_rows[32 * q : 32 * q + 4, :],
-                    )
-
-            work = ctx.enter_context(tc.tile_pool(name="work", bufs=2))
-            lift_sb = work.tile([P, GROUPS, PACK], F32, name="lift_sb", bufs=1)
-            gain_sb = work.tile([P, GROUPS, PACK], F32, name="gain_sb", bufs=1)
-            tune_sb = work.tile([P, GROUPS, PACK], F32, name="tune_sb", bufs=1)
-            wgs_first = work.tile([P, S], F32, name="wgs_first", bufs=1)
-            wgs_rest = work.tile([P, PACK - 1, S], F32, name="wgs_rest", bufs=1)
+            table_rows = head.tile([P, T // 4], I32, name="table_rows")
+            nc.sync.dma_start(pick[:], offs)
+            for q in range(4):
+                nc.sync.dma_start(
+                    out=table_rows[32 * q : 32 * q + 4, :], in_=tab_scales[0, 4 * q : 4 * q + 4, :].bitcast(I32),
+                )
+            nc.sync.dma_start(out=w2_raw[:].bitcast(I32), in_=w2_words[0].bitcast(I32))
+            nc.sync.dma_start(out=table[:], in_=tab_words[0].rearrange("p t i -> p (t i)").bitcast(I32))
+            w1_first = load_w1(0, head)
+            for q in range(4):
+                nc.sync.dma_start(
+                    out=w2_plane_raw[32 * q : 32 * q + 4, :].bitcast(I32),
+                    in_=w2_scales[0, 4 * q : 4 * q + 4, :].bitcast(I32),
+                )
+            nc.sync.dma_start(out=lift_sb[:], in_=lift.rearrange("(b p t) -> p b t", p=P, t=PACK))
+            load_page(0)
             nc.sync.dma_start(out=gain_sb[:], in_=gain.rearrange("(b p t) -> p b t", p=P, t=PACK))
             for q in range(4):
                 nc.sync.dma_start(out=wgs_first[32 * q : 32 * q + 32, :], in_=wgs_rows[:, 0, :])
-            nc.sync.dma_start(out=lift_sb[:], in_=lift.rearrange("(b p t) -> p b t", p=P, t=PACK))
-            load_page(0)
+            nc.sync.dma_start(put[:], offs2)
+            nc.sync.dma_start(recall[:], offs3)
             nc.sync.dma_start(out=tune_sb[:], in_=tune.rearrange("(b p t) -> p b t", p=P, t=PACK))
             load_page(1)
-            raws = {1: load_w1(1, work)}
             for q in range(4):
                 nc.sync.dma_start(out=wgs_rest[32 * q : 32 * q + 32, :, :], in_=wgs_rows[:, 1:PACK, :])
+            raws = {1: load_w1(1, work)}
+            nc.sync.dma_start(filed[:], offs4)
 
+            for q in range(4):
+                nc.vector.tensor_copy(
+                    out=table_plane[32 * q : 32 * q + 4, :].bitcast(I32), in_=table_rows[32 * q : 32 * q + 4, :],
+                )
             for b in range(GROUPS):
                 cols = slice(2 * b * PASS, 2 * (b + 1) * PASS)
                 nc.vector.tensor_copy(
@@ -184,9 +185,8 @@ def tile_list_reed_block_filing_kernel(
         def read(i):
             b, t = divmod(i, PACK)
             sig = work.tile([P, S], F32, name="sig", bufs=1)
-            if i > 0:
+            if i >= EARLY:
                 beat_sb = work.tile([P, S], F32, name="beat_sb")
-            lifted = work.tile([P, S + BANK], F32, name="lifted", bufs=3, align_bytes=64)
             for h in range(HALVES):
                 pitch = psum.tile([P, BANK], F32, name="pitch")
                 beat = psum.tile([P, BANK], F32, name="beat")
@@ -205,56 +205,69 @@ def tile_list_reed_block_filing_kernel(
                     start=True, stop=True,
                 )
                 nc.scalar.activation(out=sig[:, h * BANK : (h + 1) * BANK], in_=pitch[:], func=ACT.Sigmoid)
-                readings[i, h] = pitch
-                if i == 0:
-                    nc.vector.scalar_tensor_tensor(
-                        out=lifted[:, h * S : h * S + BANK], in0=sig[:, h * BANK : (h + 1) * BANK],
-                        scalar=lift_sb[:, b, t : t + 1], in1=beat[:], op0=ALU.mult, op1=ALU.subtract,
-                    )
-                else:
+                readings[i, h] = (pitch, beat)
+                if i >= EARLY:
                     nc.scalar.copy(out=beat_sb[:, h * BANK : (h + 1) * BANK], in_=beat[:])
-            if i > 0:
+            if i >= EARLY:
                 raised = work.tile([P, S], F32, name="raised")
                 nc.scalar.activation(out=raised[:], in_=sig[:], func=ACT.Copy, scale=lift_sb[:, b, t : t + 1])
+                readings[i, "terms"] = (raised, beat_sb)
+            else:
+                readings[i, "terms"] = sig
+
+        def lift_slice(i):
+            b, t = divmod(i, PACK)
+            lifted = scratch[(i + 1) % 2][:, S:]
+            if i >= EARLY:
+                raised, beat_sb = readings[i, "terms"]
                 nc.gpsimd.tensor_tensor(
                     out=lifted[:].rearrange("p (h c) -> p h c", c=BANK)[:, 0:3:2, :],
                     in0=raised[:].rearrange("p (h c) -> p h c", c=BANK),
                     in1=beat_sb[:].rearrange("p (h c) -> p h c", c=BANK), op=ALU.subtract,
                 )
-            readings[i, "lifted"] = lifted
+            else:
+                for h in range(HALVES):
+                    nc.vector.scalar_tensor_tensor(
+                        out=lifted[:, h * S : h * S + BANK], in0=readings[i, "terms"][:, h * BANK : (h + 1) * BANK],
+                        scalar=lift_sb[:, b, t : t + 1], in1=readings[i, h][1][:], op0=ALU.mult, op1=ALU.subtract,
+                    )
+
+        def weigh(i):
+            b, t = divmod(i, PACK)
             weight = work.tile([P, S], F32, name="weight")
+            readings[i] = weight
             dealt = wgs_first[:] if t == 0 else wgs_rest[:, t - 1, :]
-            if i < 2:
-                nc.vector.tensor_scalar(
-                    out=weight[:], in0=dealt, scalar1=gain_sb[:, b, t : t + 1], scalar2=None, op0=ALU.mult,
+            if i < EARLY:
+                engine = nc.gpsimd if i == 0 else nc.vector
+                engine.tensor_scalar(
+                    out=weight[:], in0=dealt, scalar1=gain_sb[:, b, t : t + 1], scalar2=0.0, op0=ALU.mult, op1=ALU.add,
                 )
             else:
                 nc.scalar.activation(out=weight[:], in_=dealt, func=ACT.Copy, scale=gain_sb[:, b, t : t + 1])
-            readings[i] = weight
 
         def combine(i):
-            larger = work.tile([P, S], F32, name="larger", bufs=1)
-            lifted = readings[i, "lifted"]
+            larger = scratch[i % 2][:, 0:S]
+            lifted = scratch[(i + 1) % 2][:, S:]
             for h in range(HALVES):
                 nc.vector.tensor_tensor(
-                    out=larger[:, h * BANK : (h + 1) * BANK], in0=readings[i, h][:],
+                    out=larger[:, h * BANK : (h + 1) * BANK], in0=readings[i, h][0][:],
                     in1=lifted[:, h * S : h * S + BANK], op=ALU.max,
                 )
-            return larger, lifted
 
-        def replace(i, larger):
+        def replace(i):
             nc.vector.tensor_tensor(
-                out=pages[i][:].indirect(put[:]), in0=larger[:], in1=readings[i][:], op=ALU.mult,
+                out=pages[i][:].indirect(put[:]), in0=scratch[i % 2][:, 0:S], in1=readings[i][:], op=ALU.mult,
             )
 
         planes = {}
 
         def fetch(i, fetched, c0, c1):
+            nc.vector.tensor_copy(out=fetched, in_=pages[i][:].indirect(recall[:, c0 // 16 : c1 // 16]))
+
+        def tune_fetched(i, fetched, c0, c1):
             b, t = divmod(i, PACK)
             if t == 0 and c0 == 0:
                 planes[b] = work.tile([P, PACK, RECALL], BF16, name="planes")
-            part = recall[:, c0 // 16 : c1 // 16]
-            nc.vector.tensor_copy(out=fetched, in_=pages[i][:].indirect(part))
             nc.scalar.activation(
                 out=planes[b][:, t, c0:c1], in_=fetched, func=ACT.Copy, scale=tune_sb[:, b, t : t + 1],
             )
@@ -262,11 +275,11 @@ def tile_list_reed_block_filing_kernel(
         def fetch_now(i, spent):
             width = CHUNKS[0][1] if i >= SLICES - PACK else RECALL
             fetch(i, spent[:, 0:width], 0, width)
+            tune_fetched(i, spent[:, 0:width], 0, width)
 
-        def quantise_x(b, c0, c1, pool, tag):
+        def quantise_x(b, c0, c1, woven):
             h, lo = divmod(c0, BANK)
             width = c1 - c0
-            woven = pool.tile([P, PACK * width], BF16, name=tag, align_bytes=64)
             nc.scalar.copy(
                 out=woven[:].rearrange("p (c i t) -> p c t i", i=PACK, t=PACK),
                 in_=planes[b][:, :, c0:c1].rearrange("p t (c i) -> p c t i", i=PACK),
@@ -309,63 +322,80 @@ def tile_list_reed_block_filing_kernel(
         loads = {
             2: lambda: load_w3(0),
             3: lambda: load_w3(1),
-            4: lambda: load_w1(2, work),
+            5: lambda: load_w1(2, work),
             7: lambda: load_w3(2),
         }
         jobs = {
-            1: lambda: quantise_w1(1, raws[1]),
-            2: lambda: quantise_w3(0, raws[2]),
-            3: lambda: quantise_w3(1, raws[3]),
-            4: lambda: quantise_w1(2, raws[4]),
-            5: lambda: quantise_x(0, 0, BANK, work, "x_woven"),
-            6: lambda: quantise_x(0, BANK, RECALL, work, "x_woven"),
-            7: lambda: quantise_w3(2, raws[7]),
-            9: lambda: quantise_x(1, 0, BANK, work, "x_woven"),
-            10: lambda: quantise_x(1, BANK, RECALL, work, "x_woven"),
+            1: lambda room: quantise_w1(1, raws[1], room),
+            2: lambda room: quantise_w3(0, raws[2], room),
+            3: lambda room: quantise_w3(1, raws[3], room),
+            4: lambda room: quantise_x(0, 0, BANK, room),
+            5: lambda room: quantise_w1(2, raws[5], room),
+            6: lambda room: quantise_x(0, BANK, RECALL, room),
+            7: lambda room: quantise_w3(2, raws[7], room),
+            8: lambda room: quantise_x(1, 0, BANK, room),
+            9: lambda room: quantise_x(1, BANK, RECALL, room),
         }
+        last = GROUPS - 1
         read(0)
+        lift_slice(0)
+        weigh(0)
+        read(1)
         for i in range(SLICES):
             b, t = divmod(i, PACK)
             if i + 1 in loads:
                 raws[i + 1] = loads[i + 1]()
             if i + 2 < SLICES:
                 load_page(i + 2)
-            if i + 1 < SLICES:
-                read(i + 1)
-            if i in jobs:
-                jobs[i]()
-            larger, lifted = combine(i)
+            combine(i)
             if i > 0:
-                fetch_now(i - 1, lifted)
-            replace(i, larger)
+                fetch_now(i - 1, scratch[(i + 1) % 2][:, S:])
+            if i + 1 < EARLY:
+                lift_slice(i + 1)
+            replace(i)
+            if i + 1 < EARLY:
+                weigh(i + 1)
+            if i in jobs:
+                jobs[i](scratch[(i + 1) % 2][:, ROOM : ROOM + S].bitcast(BF16))
+            if i + 2 < SLICES:
+                read(i + 2)
+                lift_slice(i + 2)
+                weigh(i + 2)
             if t == 2:
                 nc.sync.dma_start(out=filing[b][:], in_=page1[b * P : (b + 1) * P, :])
             if i == PACK - 1:
                 nc.sync.dma_start(out=wgo_sb[:], in_=wgo)
 
-        last = GROUPS - 1
-        fetched = work.tile([P, S + BANK], F32, name="lifted", bufs=3, align_bytes=64)
-        fetch_now(SLICES - 1, fetched)
         first, second, third = CHUNKS
-        quantise_x(last, *first, late, "first_woven")
-        held = work.tile([P, PACK, second[1] - second[0]], F32, name="larger", bufs=1)
+        fetched = late.tile([P, first[1]], F32, name="fetched")
+        fetch_now(SLICES - 1, fetched)
+        woven = late.tile([P, PACK * first[1]], BF16, name="first_woven", align_bytes=64)
+        quantise_x(last, *first, woven[:])
+        width = second[1] - second[0]
         for t in range(PACK):
-            fetch(last * PACK + t, held[:, t, :], *second)
-        held = late.tile([P, 2, third[1] - third[0]], F32, name="first_woven", align_bytes=64)
+            held = scratch[(SLICES - 1) % 2][:, t * width : (t + 1) * width]
+            fetch(last * PACK + t, held, *second)
+            tune_fetched(last * PACK + t, held, *second)
+        pairs = [late.tile([P, 2, third[1] - third[0]], F32, name="first_woven", align_bytes=64)]
         for t in range(2):
-            fetch(last * PACK + t, held[:, t, :], *third)
+            fetch(last * PACK + t, pairs[0][:, t, :], *third)
         scores = [(n, c0, c1) for c0, c1 in CHUNKS for n in range(N // P)]
         banks = ("pitch", "beat")
         rest = reduce_scores(*scores[0], banks[0], late, "first_turns")
-        quantise_x(last, *second, work, "x_woven")
-        held = late.tile([P, 2, third[1] - third[0]], F32, name="first_turns")
+        woven = late.tile([P, PACK * width], BF16, name="second_woven", align_bytes=64)
+        quantise_x(last, *second, woven[:])
+        pairs.append(late.tile([P, 2, third[1] - third[0]], F32, name="first_turns"))
         for t in range(2):
-            fetch(last * PACK + 2 + t, held[:, t, :], *third)
+            fetch(last * PACK + 2 + t, pairs[1][:, t, :], *third)
         for g, (n, c0, c1) in enumerate(scores):
-            if g == N // P - 1:
-                quantise_x(last, *third, work, "x_woven")
+            if g == 2 * (N // P) - 2:
+                woven = late.tile([P, PACK * (third[1] - third[0])], BF16, name="third_woven", align_bytes=64)
+                quantise_x(last, *third, woven[:])
             ahead = reduce_scores(*scores[g + 1], banks[(g + 1) % 2], work, "beat_sb") if g + 1 < len(scores) else None
             file_scores(n, c0, c1, rest)
+            if g < len(pairs):
+                for t in range(2):
+                    tune_fetched(last * PACK + 2 * g + t, pairs[g][:, t, :], *third)
             if c1 == RECALL:
                 nc.sync.dma_start(out=out[n * P : (n + 1) * P, :], in_=filing[n][:])
             rest = ahead

import math
from contextlib import ExitStack

import concourse.mybir as mybir

K, T, S, H, T2, RECALL, N = 512, 4096, 1024, 1536, 2048, 1024, 384
FLOPS = 2 * (2 * K * H * S) + 2 * H * N * RECALL

F32 = mybir.dt.float32
BF16 = mybir.dt.bfloat16
I32 = mybir.dt.int32
U32 = mybir.dt.uint32
U16 = mybir.dt.uint16
U8 = mybir.dt.uint8
FP8X4 = mybir.dt.float8_e4m3fn_x4
FP4X4 = mybir.dt.float4_e2m1fn_x4
ALU = mybir.AluOpType
ACT = mybir.ActivationFunctionType

P = 128
PACK = 4
PASS = P * PACK
BANK = 512
HALVES = S // BANK
GROUPS = H // PASS
SLICES = GROUPS * PACK
LIST_COLS = BANK // 16
CHUNKS = ((0, 256), (256, 512), (512, 1024))
EARLY = 2
ROOM = 384
ROUNDER = 1.5 * 2.0**23


def tile_list_reed_block_filing_kernel(
    tc, tab_words, tab_scales, offs, offs2, offs3, offs4, w1, w2_words, w2_scales,
    lift, gain, wgs, page0, tune, w3, wgo, page1, out,
):
    nc = tc.nc
    with ExitStack() as ctx:
        lists = ctx.enter_context(tc.tile_pool(name="lists", bufs=1))
        keep = ctx.enter_context(tc.tile_pool(name="keep", bufs=1))
        work = ctx.enter_context(tc.tile_pool(name="work", bufs=2))
        psum = ctx.enter_context(tc.psum_pool(name="psum", bufs=4))

        pick = lists.tile([P, S // 16], U16, name="pick")
        put = lists.tile([P, S // 16], U16, name="put")
        recall = lists.tile([P, RECALL // 16], U16, name="recall")
        filed = lists.tile([P, RECALL // 16], U16, name="filed")

        v_words = [keep.tile([P, BANK], U32, name="v_words%d" % h, align_bytes=64) for h in range(HALVES)]
        v_scales = [keep.tile([P, BANK], U8, name="v_scales%d" % h, align_bytes=64) for h in range(HALVES)]
        w1_codes = [keep.tile([P, PASS], U32, name="w1_codes%d" % b, align_bytes=64) for b in range(GROUPS)]
        w1_scales = [keep.tile([P, PASS], U8, name="w1_scales%d" % b, align_bytes=64) for b in range(GROUPS)]
        w2_codes = keep.tile([P, 2 * H], U8, name="w2_codes", align_bytes=64)
        w2_plane = keep.tile([P, H], U8, name="w2_plane", align_bytes=64)
        w3_codes = [keep.tile([P, N], U32, name="w3_codes%d" % b, align_bytes=64) for b in range(GROUPS)]
        w3_scales = [keep.tile([P, N], U8, name="w3_scales%d" % b, align_bytes=64) for b in range(GROUPS)]
        x_codes = {}
        x_scales = {}
        for b in range(GROUPS):
            for h in range(HALVES):
                x_codes[b, h] = keep.tile([P, BANK], U32, name="x_codes%d_%d" % (b, h), align_bytes=64)
                x_scales[b, h] = keep.tile([P, BANK], U8, name="x_scales%d_%d" % (b, h), align_bytes=64)
        lift_sb = keep.tile([P, GROUPS, PACK], F32, name="lift_sb")
        gain_sb = keep.tile([P, GROUPS, PACK], F32, name="gain_sb")
        tune_sb = keep.tile([P, GROUPS, PACK], F32, name="tune_sb")
        wgs_first = keep.tile([P, S], F32, name="wgs_first")
        wgs_rest = keep.tile([P, PACK - 1, S], F32, name="wgs_rest")
        scratch = [keep.tile([P, 2 * S + BANK], F32, name="scratch%d" % s, align_bytes=64) for s in range(2)]
        wgs_rows = wgs.rearrange("(p t) j -> p t j", t=PACK)

        pages = {}

        def load_page(i):
            b, t = divmod(i, PACK)
            pages[i] = work.tile([P, T2], F32, name="page", bufs=5)
            rows = page0[b * PASS : (b + 1) * PASS, :].rearrange("(p t) c -> p t c", t=PACK)
            nc.sync.dma_start(out=pages[i][:], in_=rows[:, t, :])

        def load_w1(b, pool):
            raw = pool.tile([P, PACK, PASS], F32, name="w_raw")
            nc.sync.dma_start(out=raw[:], in_=w1[:, b * PASS : (b + 1) * PASS].rearrange("(p j) c -> p j c", j=PACK))
            return raw

        def quantise_w1(b, raw, woven):
            nc.scalar.copy(
                out=woven[:].rearrange("p (t m j) -> p m t j", t=PACK, j=PACK),
                in_=raw[:].rearrange("p j (m t) -> p m t j", t=PACK),
            )
            nc.vector.quantize_mx(out=w1_codes[b][:].bitcast(FP8X4), scales=w1_scales[b][:], in_=woven[:])

        def quantise_w1_first(raw, pool):
            woven = pool.tile([P, PACK * PASS], BF16, name="w_woven", align_bytes=64)
            dst = woven[:].rearrange("p (t m j) -> p m t j", t=PACK, j=PACK)
            src = raw[:].rearrange("p j (m t) -> p m t j", t=PACK)
            for t0, t1 in ((0, 1), (1, 2), (2, PACK)):
                nc.scalar.copy(out=dst[:, :, t0:t1, :], in_=src[:, :, t0:t1, :])
                nc.vector.quantize_mx(
                    out=w1_codes[0][:, t0 * P : t1 * P].bitcast(FP8X4), scales=w1_scales[0][:, t0 * P : t1 * P],
                    in_=woven[:, t0 * PASS : t1 * PASS],
                )

        def load_w3(b):
            raw = work.tile([P, PACK, N], F32, name="w_raw")
            nc.sync.dma_start(out=raw[:], in_=w3[b * PASS : (b + 1) * PASS, :].rearrange("(p j) n -> p j n", j=PACK))
            return raw

        def quantise_w3(b, raw, room):
            woven = room[:, 0 : PACK * N]
            nc.scalar.copy(
                out=woven[:].rearrange("p (c i j) -> p c j i", i=PACK, j=PACK),
                in_=raw[:].rearrange("p j (c i) -> p c j i", i=PACK),
            )
            for c0, c1 in ((0, 2 * P), (2 * P, N)):
                nc.vector.quantize_mx(
                    out=w3_codes[b][:, c0:c1].bitcast(FP8X4),
                    scales=w3_scales[b][:, c0:c1],
                    in_=woven[:, PACK * c0 : PACK * c1],
                )

        with tc.tile_pool(name="head", bufs=1, side="right") as head:
            table = head.tile([P, T], I32, name="table")
            table_plane = head.tile([P, T], U8, name="table_plane")
            w2_raw = head.tile([P, 2 * H], U8, name="w2_raw")
            w2_plane_raw = head.tile([P, H], U8, name="w2_plane_raw")
            nc.vector.memset(table_plane[:].bitcast(I32), 0)
            nc.vector.memset(w2_plane_raw[:].bitcast(I32), 0)
            table_rows = head.tile([P, T // 4], I32, name="table_rows")
            nc.sync.dma_start(pick[:], offs)
            for q in range(4):
                nc.sync.dma_start(
                    out=table_rows[32 * q : 32 * q + 4, :], in_=tab_scales[0, 4 * q : 4 * q + 4, :].bitcast(I32),
                )
            nc.sync.dma_start(out=w2_raw[:].bitcast(I32), in_=w2_words[0].bitcast(I32))
            nc.sync.dma_start(out=table[:], in_=tab_words[0].rearrange("p t i -> p (t i)").bitcast(I32))
            w1_first = load_w1(0, head)
            for q in range(4):
                nc.sync.dma_start(
                    out=w2_plane_raw[32 * q : 32 * q + 4, :].bitcast(I32),
                    in_=w2_scales[0, 4 * q : 4 * q + 4, :].bitcast(I32),
                )
            nc.sync.dma_start(out=lift_sb[:], in_=lift.rearrange("(b p t) -> p b t", p=P, t=PACK))
            load_page(0)
            nc.sync.dma_start(out=gain_sb[:], in_=gain.rearrange("(b p t) -> p b t", p=P, t=PACK))
            for q in range(4):
                nc.sync.dma_start(out=wgs_first[32 * q : 32 * q + 32, :], in_=wgs_rows[:, 0, :])
            nc.sync.dma_start(put[:], offs2)
            nc.sync.dma_start(recall[:], offs3)
            nc.sync.dma_start(out=tune_sb[:], in_=tune.rearrange("(b p t) -> p b t", p=P, t=PACK))
            load_page(1)
            for q in range(4):
                nc.sync.dma_start(out=wgs_rest[32 * q : 32 * q + 32, :, :], in_=wgs_rows[:, 1:PACK, :])
            raws = {1: load_w1(1, work)}
            nc.sync.dma_start(filed[:], offs4)

            for q in range(4):
                nc.vector.tensor_copy(
                    out=table_plane[32 * q : 32 * q + 4, :].bitcast(I32), in_=table_rows[32 * q : 32 * q + 4, :],
                )
            for b in range(GROUPS):
                cols = slice(2 * b * PASS, 2 * (b + 1) * PASS)
                nc.vector.tensor_copy(
                    out=w2_codes[:, cols].rearrange("p (t m e) -> p t m e", t=PACK, e=2),
                    in_=w2_raw[:, cols].rearrange("p (m t e) -> p t m e", t=PACK, e=2),
                )
                cols = slice(b * PASS, (b + 1) * PASS)
                nc.vector.tensor_copy(
                    out=w2_plane[:, cols].rearrange("p (t m) -> p t m", t=PACK),
                    in_=w2_plane_raw[:, cols].rearrange("p (m t) -> p t m", t=PACK),
                )

            for h in range(HALVES):
                part = pick[:, h * LIST_COLS : (h + 1) * LIST_COLS]
                nc.vector.tensor_copy(out=v_words[h][:], in_=table[:].bitcast(U32).indirect(part))
                nc.vector.tensor_copy(out=v_scales[h][:], in_=table_plane[:].indirect(part))
                if h == 0:
                    quantise_w1_first(w1_first, head)

        late = ctx.enter_context(tc.tile_pool(name="late", bufs=1, side="right"))
        filing = [late.tile([P, T2], F32, name="filing%d" % n) for n in range(N // P)]
        wgo_sb = late.tile([P, RECALL], F32, name="wgo_sb")

        readings = {}

        def read(i):
            b, t = divmod(i, PACK)
            sig = work.tile([P, S], F32, name="sig", bufs=1)
            if i >= EARLY:
                beat_sb = work.tile([P, S], F32, name="beat_sb")
            for h in range(HALVES):
                pitch = psum.tile([P, BANK], F32, name="pitch")
                beat = psum.tile([P, BANK], F32, name="beat")
                nc.tensor.matmul_mx(
                    out=pitch[:],
                    lhsT=w1_codes[b][:, t * P : (t + 1) * P].bitcast(FP8X4),
                    lhsT_scale=w1_scales[b][:, t * P : (t + 1) * P],
                    rhs=v_words[h][:].bitcast(FP8X4), rhs_scale=v_scales[h][:],
                    start=True, stop=True,
                )
                nc.tensor.matmul_mx(
                    out=beat[:],
                    lhsT=w2_codes[:, 2 * i * P : 2 * (i + 1) * P].bitcast(FP4X4),
                    lhsT_scale=w2_plane[:, i * P : (i + 1) * P],
                    rhs=v_words[h][:].bitcast(FP8X4), rhs_scale=v_scales[h][:],
                    start=True, stop=True,
                )
                nc.scalar.activation(out=sig[:, h * BANK : (h + 1) * BANK], in_=pitch[:], func=ACT.Sigmoid)
                readings[i, h] = (pitch, beat)
                if i >= EARLY:
                    nc.scalar.copy(out=beat_sb[:, h * BANK : (h + 1) * BANK], in_=beat[:])
            if i >= EARLY:
                raised = work.tile([P, S], F32, name="raised")
                nc.scalar.activation(out=raised[:], in_=sig[:], func=ACT.Copy, scale=lift_sb[:, b, t : t + 1])
                readings[i, "terms"] = (raised, beat_sb)
            else:
                readings[i, "terms"] = sig

        def lift_slice(i):
            b, t = divmod(i, PACK)
            lifted = scratch[(i + 1) % 2][:, S:]
            if i >= EARLY:
                raised, beat_sb = readings[i, "terms"]
                nc.gpsimd.tensor_tensor(
                    out=lifted[:].rearrange("p (h c) -> p h c", c=BANK)[:, 0:3:2, :],
                    in0=raised[:].rearrange("p (h c) -> p h c", c=BANK),
                    in1=beat_sb[:].rearrange("p (h c) -> p h c", c=BANK), op=ALU.subtract,
                )
            else:
                for h in range(HALVES):
                    nc.vector.scalar_tensor_tensor(
                        out=lifted[:, h * S : h * S + BANK], in0=readings[i, "terms"][:, h * BANK : (h + 1) * BANK],
                        scalar=lift_sb[:, b, t : t + 1], in1=readings[i, h][1][:], op0=ALU.mult, op1=ALU.subtract,
                    )

        def weigh(i):
            b, t = divmod(i, PACK)
            weight = work.tile([P, S], F32, name="weight")
            readings[i] = weight
            dealt = wgs_first[:] if t == 0 else wgs_rest[:, t - 1, :]
            if i < EARLY:
                engine = nc.gpsimd if i == 0 else nc.vector
                engine.tensor_scalar(
                    out=weight[:], in0=dealt, scalar1=gain_sb[:, b, t : t + 1], scalar2=0.0, op0=ALU.mult, op1=ALU.add,
                )
            else:
                nc.scalar.activation(out=weight[:], in_=dealt, func=ACT.Copy, scale=gain_sb[:, b, t : t + 1])

        def combine(i):
            larger = scratch[i % 2][:, 0:S]
            lifted = scratch[(i + 1) % 2][:, S:]
            for h in range(HALVES):
                nc.vector.tensor_tensor(
                    out=larger[:, h * BANK : (h + 1) * BANK], in0=readings[i, h][0][:],
                    in1=lifted[:, h * S : h * S + BANK], op=ALU.max,
                )

        def replace(i):
            nc.vector.tensor_tensor(
                out=pages[i][:].indirect(put[:]), in0=scratch[i % 2][:, 0:S], in1=readings[i][:], op=ALU.mult,
            )

        planes = {}

        def fetch(i, fetched, c0, c1):
            nc.vector.tensor_copy(out=fetched, in_=pages[i][:].indirect(recall[:, c0 // 16 : c1 // 16]))

        def tune_fetched(i, fetched, c0, c1):
            b, t = divmod(i, PACK)
            if t == 0 and c0 == 0:
                planes[b] = work.tile([P, PACK, RECALL], BF16, name="planes")
            nc.scalar.activation(
                out=planes[b][:, t, c0:c1], in_=fetched, func=ACT.Copy, scale=tune_sb[:, b, t : t + 1],
            )

        def fetch_now(i, spent):
            width = CHUNKS[0][1] if i >= SLICES - PACK else RECALL
            fetch(i, spent[:, 0:width], 0, width)
            tune_fetched(i, spent[:, 0:width], 0, width)

        def quantise_x(b, c0, c1, woven):
            h, lo = divmod(c0, BANK)
            width = c1 - c0
            nc.scalar.copy(
                out=woven[:].rearrange("p (c i t) -> p c t i", i=PACK, t=PACK),
                in_=planes[b][:, :, c0:c1].rearrange("p t (c i) -> p c t i", i=PACK),
            )
            nc.vector.quantize_mx(
                out=x_codes[b, h][:, lo : lo + width].bitcast(FP8X4), scales=x_scales[b, h][:, lo : lo + width],
                in_=woven[:],
            )

        def reduce_scores(n, c0, c1, bank, pool, tag):
            h, lo = divmod(c0, BANK)
            width = c1 - c0
            z = psum.tile([P, width], F32, name=bank)
            for b in range(GROUPS):
                nc.tensor.matmul_mx(
                    out=z[:],
                    lhsT=w3_codes[b][:, n * P : (n + 1) * P].bitcast(FP8X4),
                    lhsT_scale=w3_scales[b][:, n * P : (n + 1) * P],
                    rhs=x_codes[b, h][:, lo : lo + width].bitcast(FP8X4), rhs_scale=x_scales[b, h][:, lo : lo + width],
                    start=(b == 0), stop=(b == GROUPS - 1),
                )
            turns_raw = work.tile([P, width], U32, name="raised")
            nc.scalar.activation(out=turns_raw[:], in_=z[:], func=ACT.Copy, scale=1.0 / (2.0 * math.pi), bias=ROUNDER)
            turns = pool.tile([P, width], F32, name=tag)
            nc.scalar.activation(out=turns[:], in_=turns_raw[:], func=ACT.Copy, bias=-ROUNDER)
            rest = late.tile([P, width], F32, name="rest", bufs=3)
            nc.vector.scalar_tensor_tensor(
                out=rest[:], in0=z[:], scalar=1.0 / (2.0 * math.pi), in1=turns[:], op0=ALU.mult, op1=ALU.subtract,
            )
            return rest

        def file_scores(n, c0, c1, rest):
            y = work.tile([P, c1 - c0], F32, name="weight")
            nc.scalar.activation(out=y[:], in_=rest[:], func=ACT.Sin, scale=2.0 * math.pi)
            nc.vector.tensor_tensor(
                out=filing[n][:].indirect(filed[:, c0 // 16 : c1 // 16]),
                in0=y[:], in1=wgo_sb[:, c0:c1], op=ALU.mult,
            )

        loads = {
            2: lambda: load_w3(0),
            3: lambda: load_w3(1),
            5: lambda: load_w1(2, work),
            7: lambda: load_w3(2),
        }
        jobs = {
            1: lambda room: quantise_w1(1, raws[1], room),
            2: lambda room: quantise_w3(0, raws[2], room),
            3: lambda room: quantise_w3(1, raws[3], room),
            4: lambda room: quantise_x(0, 0, BANK, room),
            5: lambda room: quantise_w1(2, raws[5], room),
            6: lambda room: quantise_x(0, BANK, RECALL, room),
            7: lambda room: quantise_w3(2, raws[7], room),
            8: lambda room: quantise_x(1, 0, BANK, room),
            9: lambda room: quantise_x(1, BANK, RECALL, room),
        }
        last = GROUPS - 1
        read(0)
        lift_slice(0)
        weigh(0)
        read(1)
        for i in range(SLICES):
            b, t = divmod(i, PACK)
            if i + 1 in loads:
                raws[i + 1] = loads[i + 1]()
            if i + 2 < SLICES:
                load_page(i + 2)
            combine(i)
            if i > 0:
                fetch_now(i - 1, scratch[(i + 1) % 2][:, S:])
            if i + 1 < EARLY:
                lift_slice(i + 1)
            replace(i)
            if i + 1 < EARLY:
                weigh(i + 1)
            if i in jobs:
                jobs[i](scratch[(i + 1) % 2][:, ROOM : ROOM + S].bitcast(BF16))
            if i + 2 < SLICES:
                read(i + 2)
                lift_slice(i + 2)
                weigh(i + 2)
            if t == 2:
                nc.sync.dma_start(out=filing[b][:], in_=page1[b * P : (b + 1) * P, :])
            if i == PACK - 1:
                nc.sync.dma_start(out=wgo_sb[:], in_=wgo)

        first, second, third = CHUNKS
        fetched = late.tile([P, first[1]], F32, name="fetched")
        fetch_now(SLICES - 1, fetched)
        woven = late.tile([P, PACK * first[1]], BF16, name="first_woven", align_bytes=64)
        quantise_x(last, *first, woven[:])
        width = second[1] - second[0]
        for t in range(PACK):
            held = scratch[(SLICES - 1) % 2][:, t * width : (t + 1) * width]
            fetch(last * PACK + t, held, *second)
            tune_fetched(last * PACK + t, held, *second)
        pairs = [late.tile([P, 2, third[1] - third[0]], F32, name="first_woven", align_bytes=64)]
        for t in range(2):
            fetch(last * PACK + t, pairs[0][:, t, :], *third)
        scores = [(n, c0, c1) for c0, c1 in CHUNKS for n in range(N // P)]
        banks = ("pitch", "beat")
        rest = reduce_scores(*scores[0], banks[0], late, "first_turns")
        woven = late.tile([P, PACK * width], BF16, name="second_woven", align_bytes=64)
        quantise_x(last, *second, woven[:])
        pairs.append(late.tile([P, 2, third[1] - third[0]], F32, name="first_turns"))
        for t in range(2):
            fetch(last * PACK + 2 + t, pairs[1][:, t, :], *third)
        for g, (n, c0, c1) in enumerate(scores):
            if g == 2 * (N // P) - 2:
                woven = late.tile([P, PACK * (third[1] - third[0])], BF16, name="third_woven", align_bytes=64)
                quantise_x(last, *third, woven[:])
            ahead = reduce_scores(*scores[g + 1], banks[(g + 1) % 2], work, "beat_sb") if g + 1 < len(scores) else None
            file_scores(n, c0, c1, rest)
            if g < len(pairs):
                for t in range(2):
                    tune_fetched(last * PACK + 2 * g + t, pairs[g][:, t, :], *third)
            if c1 == RECALL:
                nc.sync.dma_start(out=out[n * P : (n + 1) * P, :], in_=filing[n][:])
            rest = ahead
